import numpy as np
import ml_dtypes


def mxq(x, axis, fmt="e4m3"):
    dtype, down = {"e4m3": (ml_dtypes.float8_e4m3fn, 7), "e5m2": (ml_dtypes.float8_e5m2, 14)}[fmt]
    v = np.moveaxis(np.asarray(x, np.float32).astype(ml_dtypes.bfloat16).astype(np.float64), axis, -1)
    blocks = v.reshape(v.shape[:-1] + (-1, 32))
    amax = np.abs(blocks).max(-1, keepdims=True)
    byte = np.maximum(np.where(amax > 0, np.frexp(amax)[1] - 1 + 127, 0) - down, 1)
    scale = np.exp2(byte - 127.0)
    codes = (blocks / scale).astype(np.float32).astype(dtype).astype(np.float64)
    return np.moveaxis((codes * scale).reshape(v.shape), -1, axis)


WIDE = False


def mx_kscale(k):
    if not WIDE:
        return np.ones(k)
    levels = np.array([10, -10, 5, -5, 0])
    if k % 512:
        return np.exp2(np.random.permutation(np.resize(levels, k // 32))).repeat(32)
    a = np.empty((k // 512, 16))
    for p in range(k // 512):
        a[p, :8] = np.random.permutation(np.resize(levels, 8))
        for g in range(8):
            far = levels[np.abs(levels - a[p, g]) >= 10]
            a[p, g + 8] = far[np.random.randint(len(far))]
    return np.exp2(a.ravel()).repeat(32)


def f64(x):
    return np.asarray(x).astype(np.float64)


def striped(idx):
    return np.tile(idx.reshape(-1, 16).T, (8, 1)).astype(np.uint16)


def unstriped(offs):
    return offs[:16].T.reshape(-1).astype(np.int64)


E2M1 = np.array([0.0, 0.5, 1.0, 1.5, 2.0, 3.0, 4.0, 6.0, -0.0, -0.5, -1.0, -1.5, -2.0, -3.0, -4.0, -6.0])


def pack_weight(w, fmt):
    k, n = w.shape
    w = f64(np.asarray(w, np.float32).astype(ml_dtypes.bfloat16)).reshape(k // 32, 32, n)
    amax = np.abs(w).max(1)
    if fmt == "e4m3":
        byte = np.frexp(amax)[1] - 1 + 127 - 7
    else:
        mant, ex = np.frexp(amax / 6.0)
        byte = np.where(mant > 0.5, ex, ex - 1) + 127
    byte = np.clip(np.where(amax > 0, byte, 1), 1, 254)
    scaled = (w * np.exp2(127.0 - byte)[:, None, :]).reshape(k, n).astype(np.float32)
    by_word = np.ascontiguousarray(scaled.reshape(k // 512, 128, 4, n).transpose(0, 1, 3, 2))
    if fmt == "e4m3":
        words = by_word.astype(ml_dtypes.float8_e4m3fn).view(np.uint8)
    else:
        c = by_word.astype(ml_dtypes.float4_e2m1fn).view(np.uint8) & 0xF
        words = (c[..., 0::2] | (c[..., 1::2] << 4)).reshape(k // 512, 128, 2 * n)
    return np.ascontiguousarray(words), np.ascontiguousarray(byte.astype(np.uint8).reshape(k // 512, 16, n))


def unpack_weight(words, scales, fmt):
    g, _, n = scales.shape
    words = np.ascontiguousarray(words).reshape(g, 128, n, -1)
    if fmt == "e4m3":
        vals = words.view(ml_dtypes.float8_e4m3fn).astype(np.float64)
    else:
        nib = np.empty((g, 128, n, 4), np.uint8)
        nib[..., 0::2] = words & 0xF
        nib[..., 1::2] = words >> 4
        vals = E2M1[nib]
    vals = vals * np.repeat(np.exp2(scales.astype(np.float64) - 127.0), 8, axis=1)[..., None]
    return vals.transpose(0, 1, 3, 2).reshape(g * 512, n)


def gelu(v):
    return 0.5 * v * (1.0 + np.tanh(np.sqrt(2.0 / np.pi) * (v + 0.044715 * v**3)))


K, H, T, S, P = 1024, 512, 4096, 1024, 512


def setup_inputs():
    n = np.random.standard_normal
    s = mx_kscale(K)[:, None]
    u = mx_kscale(H)[:, None]
    tab_words, tab_scales = pack_weight(n((K, T)) * s, "e4m3")
    w1 = 0.55 * n((K, H)) / np.sqrt(K) / s
    w2 = 1.5 * n((K, H)) / np.sqrt(K) / s * u.T
    w3 = 0.6 * n((K, H)) / np.sqrt(K) / s * u.T
    w2_words, w2_scales = pack_weight(w2, "e2m1")
    gain = np.exp(0.3 * n(H)) / np.sqrt(H) / u[:, 0] ** 2
    return {
        "tab_words": tab_words, "tab_scales": tab_scales,
        "offs": striped(np.random.permutation(T)[:S]),
        "pos1": striped(np.random.permutation(S)[:P]),
        "pos2": striped(np.random.permutation(S)[:P]),
        "w1": w1.astype(np.float32),
        "w2_words": w2_words, "w2_scales": w2_scales,
        "w3": w3.astype(np.float32),
        "gain": gain.astype(np.float32),
        "board": (0.7 * n(P)).astype(np.float32),
    }


def reference(tab_words, tab_scales, offs, pos1, pos2, w1, w2_words, w2_scales, w3, gain, board):
    v = unpack_weight(tab_words, tab_scales, "e4m3")[:, unstriped(offs)]
    w2 = unpack_weight(w2_words, w2_scales, "e2m1")
    a = mxq(f64(w1), 0, "e4m3").T @ v
    b = w2.T @ v
    d = mxq(f64(w3), 0, "e4m3").T @ v
    h = np.sin(a) * b + d
    x1 = h[:, unstriped(pos1)]
    x2 = np.abs(h[:, unstriped(pos2)]) * f64(gain)[:, None]
    e = mxq(x1, 0, "e4m3").T @ mxq(x2, 0, "e4m3")
    return np.tanh(e + f64(board)[None, :])

@@ -1,0 +1,271 @@
+import math
+from contextlib import ExitStack
+
+import concourse.mybir as mybir
+
+K, H, T, S, NP = 1024, 512, 4096, 1024, 512
+FLOPS = 3 * 2 * K * H * S + 2 * H * NP * NP
+
+F32 = mybir.dt.float32
+BF16 = mybir.dt.bfloat16
+I32 = mybir.dt.int32
+U32 = mybir.dt.uint32
+U16 = mybir.dt.uint16
+U8 = mybir.dt.uint8
+FP8X4 = mybir.dt.float8_e4m3fn_x4
+FP4X4 = mybir.dt.float4_e2m1fn_x4
+ACT = mybir.ActivationFunctionType
+ALU = mybir.AluOpType
+
+P = 128
+PACK = 4
+K_PASS = P * PACK
+PASSES = K // K_PASS
+BANK = 512
+HALVES = S // BANK
+ROUND = 1.5 * 2.0**23
+TWO_PI = 2.0 * math.pi
+W3_ENGINE = "scalar"
+V_TURNS = 0
+
+
+def tile_list_clue_association_scores_kernel(
+    tc, tab_words, tab_scales, offs, pos1, pos2, w1, w2_words, w2_scales, w3, gain, board, out
+):
+    nc = tc.nc
+    with ExitStack() as ctx:
+        keep = ctx.enter_context(tc.tile_pool(name="keep", bufs=1))
+        reuse = ctx.enter_context(tc.tile_pool(name="reuse", bufs=1))
+        ring = ctx.enter_context(tc.tile_pool(name="ring", bufs=3))
+        psum = ctx.enter_context(tc.psum_pool(name="psum", bufs=1))
+
+        def held(shape, dtype, name, tag=""):
+            return keep.tile(shape, dtype, name=name, tag=tag, align_bytes=64)
+
+        offs_sb = held([P, S // 16], U16, "offs_sb")
+        pos1_sb = held([P, NP // 16], U16, "pos1_sb")
+        pos2_sb = held([P, NP // 16], U16, "pos2_sb")
+        tsc_sb = reuse.tile([P, T], U8, name="tsc_sb", offset=15 * 1024)
+        tsc_pick = held([P, S], U8, "tsc_pick")
+        v_scale = [held([P, S], U8, f"v_scale{a}") for a in range(PASSES)]
+        v_codes = [[held([P, BANK], U32, f"v_codes{a}_{hf}") for hf in range(HALVES)] for a in range(PASSES)]
+        w_raw = {}
+        pairs = [(n, a) for n in ("w1", "w3") for a in range(PASSES)]
+        w_bf = {(n, a): held([P, H * PACK], BF16, f"{n}_bf{a}") for n, a in pairs}
+        w_codes = {(n, a): held([P, H], U32, f"{n}_codes{a}") for n, a in pairs}
+        w_scale = {(n, a): held([P, H], U8, f"{n}_scale{a}") for n, a in pairs}
+        w2_codes = held([P, PASSES, 2 * H], U8, "w2_codes")
+        w2_scale = held([P, PASSES, H], U8, "w2_scale")
+        h_sb = [held([P, S], F32, f"h_sb{t}") for t in range(PACK)]
+        x1_rows = held([P, PACK, NP], BF16, "x1_rows")
+        x2_rows = held([P, PACK, NP], BF16, "x2_rows")
+        x2_bf = held([P, NP * PACK], BF16, "x2_bf")
+        x2_codes = held([P, NP], U32, "x2_codes")
+        x2_scale = held([P, NP], U8, "x2_scale")
+
+        nc.vector.memset(tsc_sb[32:64, :].bitcast(I32), 0)
+        nc.vector.memset(tsc_sb[64:P, :].bitcast(I32), 0)
+        nc.gpsimd.memset(w2_scale[:].bitcast(I32), 0)
+        for a in range(PASSES):
+            nc.gpsimd.memset(v_scale[a][:].bitcast(I32), 0)
+        nc.sync.dma_start(offs_sb[:], offs)
+        nc.sync.dma_start(out=tsc_sb[0:32, :].bitcast(I32), in_=tab_scales.rearrange("a q t -> (a q) t").bitcast(I32))
+        nc.sync.dma_start(pos1_sb[:], pos1)
+        nc.sync.dma_start(pos2_sb[:], pos2)
+        w_dram = {"w1": w1, "w3": w3}
+
+        def load_w(n, a):
+            rows = w_dram[n][a * K_PASS : (a + 1) * K_PASS, :]
+            nc.sync.dma_start(out=w_raw[n, a], in_=rows.rearrange("(p i) c -> p i c", i=PACK))
+
+        def load_table(a):
+            nc.sync.dma_start(out=tab_sb[a][:].bitcast(I32), in_=tab_words[a].rearrange("p n i -> p (n i)").bitcast(I32))
+
+        tab_sb = {0: reuse.tile([P, T], U32, name="tab_sb0", offset=20 * 1024)}
+        load_table(0)
+        for a in range(PASSES):
+            w_raw["w1", a] = held([P, PACK, H], F32, f"w1_raw{a}", tag=f"w1_raw{a}")[:]
+            load_w("w1", a)
+
+        nc.vector.tensor_copy(tsc_pick[:], tsc_sb[:].indirect(offs_sb[:]))
+        for a in range(PASSES):
+            for q in range(4):
+                queue = nc.gpsimd if (a == 1 and q >= 2) else nc.sync
+                first = 16 * a + 4 * q
+                queue.dma_start(
+                    out=v_scale[a][32 * q : 32 * q + 4, :].bitcast(I32),
+                    in_=tsc_pick[first : first + 4, :].bitcast(I32),
+                )
+        tab_sb[1] = reuse.tile([P, T], U32, name="tab_sb1", offset=0)
+        w2_sc_raw = held([P, PASSES, H // 4], I32, "w2_sc_raw")
+        w2_raw = reuse.tile([P, PASSES, H // 2], I32, name="w2_raw", offset=17 * 1024)
+        load_table(1)
+        nc.sync.dma_start(out=w2_raw[:], in_=w2_words.bitcast(I32).rearrange("a p c -> p a c"))
+        for q in range(4):
+            nc.gpsimd.dma_start(
+                out=w2_sc_raw[32 * q : 32 * q + 4, :, :],
+                in_=w2_scales.bitcast(I32)[:, 4 * q : 4 * q + 4, :].rearrange("a r c -> r a c"),
+            )
+
+        def gather_table(a):
+            for hf in range(HALVES):
+                cols = BANK // 16
+                nc.vector.tensor_copy(v_codes[a][hf][:], tab_sb[a][:].indirect(offs_sb[:, hf * cols : (hf + 1) * cols]))
+
+        def round_w(n, a, t0, t1, engine):
+            dst = w_bf[n, a][:].rearrange("p (t g j i) -> p t g i j", t=PACK, j=4, i=PACK)[:, t0:t1]
+            src = w_raw[n, a].rearrange("p i (g t j) -> p t g i j", t=PACK, j=4)[:, t0:t1]
+            if engine == "scalar":
+                nc.scalar.copy(out=dst, in_=src)
+            elif engine == "vector":
+                nc.vector.tensor_copy(out=dst, in_=src)
+            else:
+                nc.gpsimd.tensor_scalar(out=dst, in0=src, scalar1=1.0, scalar2=0.0, op0=ALU.mult, op1=ALU.add)
+
+        def quantize_w(n, a, t0, t1):
+            nc.vector.quantize_mx(
+                out=w_codes[n, a][:, P * t0 : P * t1].bitcast(FP8X4),
+                scales=w_scale[n, a][:, P * t0 : P * t1],
+                in_=w_bf[n, a][:, P * PACK * t0 : P * PACK * t1],
+            )
+
+        def prepare_w(n, a, t0, t1, engine):
+            round_w(n, a, t0, t1, engine)
+            quantize_w(n, a, t0, t1)
+
+        gather_table(0)
+        for a in range(PASSES):
+            prepare_w("w1", a, 0, PACK, "scalar")
+        gather_table(1)
+
+        for a in range(PASSES):
+            w_raw["w3", a] = reuse.tile([P, PACK, H], F32, name=f"w3_raw{a}", offset=20 * 1024 + a * PACK * H * 4)[:]
+            load_w("w3", a)
+        late = held([P, NP + 8 * PACK], F32, "late", tag="w1_raw1")
+        board_sb = late[:, 0:NP]
+        gain_sb = [late[:, NP + 8 * t : NP + 8 * t + 1] for t in range(PACK)]
+        with nc.allow_non_contiguous_dma(reason="one gain value a partition"):
+            for t in range(PACK):
+                nc.sync.dma_start(out=gain_sb[t], in_=gain.rearrange("(g t j) -> t g j", t=PACK, j=4)[t])
+        nc.sync.dma_start(out=board_sb, in_=board.partition_broadcast(P))
+
+        def deal_w2():
+            nc.vector.tensor_copy(
+                out=w2_codes[:].bitcast(I32).rearrange("p a (t g j) -> p a t g j", t=PACK, j=2),
+                in_=w2_raw[:].rearrange("p a (g t j) -> p a t g j", t=PACK, j=2),
+            )
+            for q in range(4):
+                rows = slice(32 * q, 32 * q + 4)
+                nc.vector.tensor_copy(
+                    out=w2_scale[rows].bitcast(I32).rearrange("p a (t g) -> p a t g", t=PACK),
+                    in_=w2_sc_raw[rows].rearrange("p a (g t) -> p a t g", t=PACK),
+                )
+
+        def product(n, t, hf, bufs):
+            acc = psum.tile([P, BANK], F32, name=f"acc_{n}", tag=f"acc_{n}", bufs=bufs)
+            for a in range(PASSES):
+                if n == "w2":
+                    lhsT = w2_codes[:, a, 2 * P * t : 2 * P * (t + 1)].bitcast(FP4X4)
+                    lhsT_scale = w2_scale[:, a, P * t : P * (t + 1)]
+                else:
+                    lhsT = w_codes[n, a][:, P * t : P * (t + 1)].bitcast(FP8X4)
+                    lhsT_scale = w_scale[n, a][:, P * t : P * (t + 1)]
+                nc.tensor.matmul_mx(
+                    out=acc[:],
+                    lhsT=lhsT,
+                    lhsT_scale=lhsT_scale,
+                    rhs=v_codes[a][hf][:].bitcast(FP8X4),
+                    rhs_scale=v_scale[a][:, hf * BANK : (hf + 1) * BANK],
+                    start=(a == 0),
+                    stop=(a == PASSES - 1),
+                )
+            return acc
+
+        def gated(t, hf, on_vector):
+            a_ps = product("w1", t, hf, 3)
+            turns_u = ring.tile([P, BANK], U32, name="turns_u")
+            nc.scalar.activation(out=turns_u[:], in_=a_ps[:], func=ACT.Copy, scale=1.0 / TWO_PI, bias=ROUND)
+            turns = ring.tile([P, BANK], F32, name="turns")
+            if on_vector:
+                nc.vector.tensor_scalar(
+                    out=turns[:], in0=turns_u[:].bitcast(I32), scalar1=-ROUND, scalar2=None, op0=ALU.add
+                )
+            else:
+                nc.scalar.activation(out=turns[:], in_=turns_u[:], func=ACT.Copy, scale=1.0, bias=-ROUND)
+            angle = ring.tile([P, BANK], F32, name="angle")
+            nc.vector.scalar_tensor_tensor(
+                out=angle[:], in0=turns[:], scalar=-TWO_PI, in1=a_ps[:], op0=ALU.mult, op1=ALU.add
+            )
+            sine = ring.tile([P, BANK], F32, name="sine")
+            nc.scalar.activation(out=sine[:], in_=angle[:], func=ACT.Sin)
+            b_ps = product("w2", t, hf, 2)
+            prod = ring.tile([P, BANK], F32, name="prod", bufs=6)
+            nc.vector.tensor_tensor(out=prod[:], in0=b_ps[:], in1=sine[:], op=ALU.mult)
+            return prod
+
+        def finish_h(t, hf, prod):
+            d_ps = product("w3", t, hf, 3)
+            nc.vector.tensor_tensor(out=h_sb[t][:, hf * BANK : (hf + 1) * BANK], in0=d_ps[:], in1=prod[:], op=ALU.add)
+
+        def pick(t):
+            picked = ring.tile([P, NP], F32, name="picked", bufs=2)
+            nc.vector.tensor_copy(picked[:], h_sb[t][:].indirect(pos2_sb[:]))
+            nc.vector.tensor_copy(x1_rows[:, t, :], h_sb[t][:].indirect(pos1_sb[:]))
+            mag = ring.tile([P, NP], F32, name="mag", tag="mag", bufs=1, align_bytes=64)
+            nc.scalar.activation(out=mag[:], in_=picked[:], func=ACT.Abs)
+            nc.scalar.activation(out=x2_rows[:, t, :], in_=mag[:], func=ACT.Copy, scale=gain_sb[t])
+
+        units = [(0, 0), (1, 0), (0, 1), (1, 1), (2, 0), (2, 1), (3, 0), (3, 1)]
+        LAG = 4
+        prods = {}
+        for i in range(len(units) + LAG):
+            if i == 0:
+                deal_w2()
+            if i < len(units):
+                prods[i] = gated(*units[i], i < V_TURNS)
+            if i == 1:
+                prepare_w("w3", 0, 0, PACK, "vector")
+            if 2 <= i < 2 + PACK:
+                prepare_w("w3", 1, i - 2, i - 1, W3_ENGINE)
+            if i >= LAG:
+                t, hf = units[i - LAG]
+                finish_h(t, hf, prods[i - LAG])
+                if hf == HALVES - 1:
+                    pick(t)
+
+        nc.vector.tensor_copy(
+            out=x2_bf[:].rearrange("p (c i t) -> p c t i", i=4, t=PACK),
+            in_=x2_rows[:].rearrange("p t (c i) -> p c t i", i=4),
+        )
+        x1_q = []
+        x1_all = ring.tile([P, NP * PACK], BF16, name="x1_all", tag="mag", bufs=1, align_bytes=64)
+        for m in range(NP // P):
+            x1_bf = x1_all[:, m * P * PACK : (m + 1) * P * PACK]
+            nc.scalar.copy(
+                out=x1_bf.rearrange("p (c i t) -> p c t i", i=4, t=PACK),
+                in_=x1_rows[:, :, m * P : (m + 1) * P].rearrange("p t (c i) -> p c t i", i=4),
+            )
+            x1_q.append(x1_bf)
+        nc.vector.quantize_mx(out=x2_codes[:].bitcast(FP8X4), scales=x2_scale[:], in_=x2_bf[:])
+        x1_mx = []
+        for m in range(NP // P):
+            x1_codes = ring.tile([P, P], U32, name="x1_codes", bufs=4, align_bytes=64)
+            x1_scale = ring.tile([P, P], U8, name="x1_scale", bufs=4, align_bytes=64)
+            nc.vector.quantize_mx(out=x1_codes[:].bitcast(FP8X4), scales=x1_scale[:], in_=x1_q[m])
+            x1_mx.append((x1_codes, x1_scale))
+        for m in range(NP // P):
+            e_ps = psum.tile([P, BANK], F32, name="acc_w1", tag="acc_w1", bufs=3)
+            nc.tensor.matmul_mx(
+                out=e_ps[:],
+                lhsT=x1_mx[m][0][:].bitcast(FP8X4),
+                lhsT_scale=x1_mx[m][1][:],
+                rhs=x2_codes[:].bitcast(FP8X4),
+                rhs_scale=x2_scale[:],
+                start=True,
+                stop=True,
+            )
+            shifted = ring.tile([P, NP], F32, name="shifted", bufs=4)
+            nc.vector.tensor_tensor(out=shifted[:], in0=e_ps[:], in1=board_sb, op=ALU.add)
+            score = ring.tile([P, NP], F32, name="score", bufs=4)
+            nc.scalar.activation(out=score[:], in_=shifted[:], func=ACT.Tanh)
+            nc.sync.dma_start(out=out[m * P : (m + 1) * P, :], in_=score[:])

@@ -25,8 +25,13 @@ BANK = 512
 HALVES = S // BANK
 ROUND = 1.5 * 2.0**23
 TWO_PI = 2.0 * math.pi
-W3_ENGINE = "scalar"
+W3_ENGINE = "gpsimd"
 V_TURNS = 0
+W3A_ENGINE = "vector"
+WARM = False
+W3A_STEP = 4
+G_ADD = ((1, 0), (2, 0), (3, 0))
+BUF_A, BUF_B, BUF_D = 3, 2, 3
 
 
 def tile_list_clue_association_scores_kernel(
@@ -45,7 +50,7 @@ def tile_list_clue_association_scores_kernel(
         offs_sb = held([P, S // 16], U16, "offs_sb")
         pos1_sb = held([P, NP // 16], U16, "pos1_sb")
         pos2_sb = held([P, NP // 16], U16, "pos2_sb")
-        tsc_sb = reuse.tile([P, T], U8, name="tsc_sb", offset=15 * 1024)
+        tsc_sb = reuse.tile([P, T], U8, name="tsc_sb", offset=15 * 1024 + 64)
         tsc_pick = held([P, S], U8, "tsc_pick")
         v_scale = [held([P, S], U8, f"v_scale{a}") for a in range(PASSES)]
         v_codes = [[held([P, BANK], U32, f"v_codes{a}_{hf}") for hf in range(HALVES)] for a in range(PASSES)]
@@ -58,11 +63,14 @@ def tile_list_clue_association_scores_kernel(
         w2_scale = held([P, PASSES, H], U8, "w2_scale")
         h_sb = [held([P, S], F32, f"h_sb{t}") for t in range(PACK)]
         x1_rows = held([P, PACK, NP], BF16, "x1_rows")
-        x2_rows = held([P, PACK, NP], BF16, "x2_rows")
         x2_bf = held([P, NP * PACK], BF16, "x2_bf")
         x2_codes = held([P, NP], U32, "x2_codes")
         x2_scale = held([P, NP], U8, "x2_scale")
 
+        if WARM:
+            warm = held([P, 16], F32, "warm")
+            nc.gpsimd.memset(warm[:, 0:1], 0.0)
+            nc.scalar.activation(out=warm[:, 8:9], in_=warm[:, 0:1], func=ACT.Silu)
         nc.vector.memset(tsc_sb[32:64, :].bitcast(I32), 0)
         nc.vector.memset(tsc_sb[64:P, :].bitcast(I32), 0)
         nc.gpsimd.memset(w2_scale[:].bitcast(I32), 0)
@@ -81,31 +89,36 @@ def tile_list_clue_association_scores_kernel(
         def load_table(a):
             nc.sync.dma_start(out=tab_sb[a][:].bitcast(I32), in_=tab_words[a].rearrange("p n i -> p (n i)").bitcast(I32))
 
-        tab_sb = {0: reuse.tile([P, T], U32, name="tab_sb0", offset=20 * 1024)}
+        def move_scale_rows(a, q):
+            first = 16 * a + 4 * q
+            nc.sync.dma_start(
+                out=v_scale[a][32 * q : 32 * q + 4, :].bitcast(I32),
+                in_=tsc_pick[first : first + 4, :].bitcast(I32),
+            )
+
+        tab_sb = {0: reuse.tile([P, T], U32, name="tab_sb0", offset=28 * 1024)}
         load_table(0)
-        for a in range(PASSES):
-            w_raw["w1", a] = held([P, PACK, H], F32, f"w1_raw{a}", tag=f"w1_raw{a}")[:]
-            load_w("w1", a)
+        w_raw["w1", 0] = held([P, PACK, H], F32, "w1_raw0")[:]
+        load_w("w1", 0)
 
         nc.vector.tensor_copy(tsc_pick[:], tsc_sb[:].indirect(offs_sb[:]))
-        for a in range(PASSES):
-            for q in range(4):
-                queue = nc.gpsimd if (a == 1 and q >= 2) else nc.sync
-                first = 16 * a + 4 * q
-                queue.dma_start(
-                    out=v_scale[a][32 * q : 32 * q + 4, :].bitcast(I32),
-                    in_=tsc_pick[first : first + 4, :].bitcast(I32),
-                )
-        tab_sb[1] = reuse.tile([P, T], U32, name="tab_sb1", offset=0)
-        w2_sc_raw = held([P, PASSES, H // 4], I32, "w2_sc_raw")
-        w2_raw = reuse.tile([P, PASSES, H // 2], I32, name="w2_raw", offset=17 * 1024)
-        load_table(1)
-        nc.sync.dma_start(out=w2_raw[:], in_=w2_words.bitcast(I32).rearrange("a p c -> p a c"))
+        moves = [(a, q) for a in range(PASSES) for q in range(4)]
+        for a, q in moves[:6]:
+            move_scale_rows(a, q)
+        w_raw["w1", 1] = reuse.tile([P, PACK, H], F32, name="w1_raw1", offset=19 * 1024)[:]
+        load_w("w1", 1)
+        for a, q in moves[6:]:
+            move_scale_rows(a, q)
+        w2_sc_raw = reuse.tile([P, PASSES, H // 4], I32, name="w2_sc_raw", offset=16 * 1024)
         for q in range(4):
-            nc.gpsimd.dma_start(
+            nc.sync.dma_start(
                 out=w2_sc_raw[32 * q : 32 * q + 4, :, :],
                 in_=w2_scales.bitcast(I32)[:, 4 * q : 4 * q + 4, :].rearrange("a r c -> r a c"),
             )
+        tab_sb[1] = reuse.tile([P, T], U32, name="tab_sb1", offset=0)
+        load_table(1)
+        w2_raw = reuse.tile([P, PASSES, H // 2], I32, name="w2_raw", offset=17 * 1024)
+        nc.sync.dma_start(out=w2_raw[:], in_=w2_words.bitcast(I32).rearrange("a p c -> p a c"))
 
         def gather_table(a):
             for hf in range(HALVES):
@@ -120,7 +133,14 @@ def tile_list_clue_association_scores_kernel(
             elif engine == "vector":
                 nc.vector.tensor_copy(out=dst, in_=src)
             else:
-                nc.gpsimd.tensor_scalar(out=dst, in0=src, scalar1=1.0, scalar2=0.0, op0=ALU.mult, op1=ALU.add)
+                nc.gpsimd.tensor_scalar(
+                    out=dst.rearrange("p t g i j -> p t g j i"),
+                    in0=src.rearrange("p t g i j -> p t g j i"),
+                    scalar1=1.0,
+                    scalar2=0.0,
+                    op0=ALU.mult,
+                    op1=ALU.add,
+                )
 
         def quantize_w(n, a, t0, t1):
             nc.vector.quantize_mx(
@@ -139,9 +159,9 @@ def tile_list_clue_association_scores_kernel(
         gather_table(1)
 
         for a in range(PASSES):
-            w_raw["w3", a] = reuse.tile([P, PACK, H], F32, name=f"w3_raw{a}", offset=20 * 1024 + a * PACK * H * 4)[:]
+            w_raw["w3", a] = reuse.tile([P, PACK, H], F32, name=f"w3_raw{a}", offset=28 * 1024 + a * PACK * H * 4)[:]
             load_w("w3", a)
-        late = held([P, NP + 8 * PACK], F32, "late", tag="w1_raw1")
+        late = reuse.tile([P, NP + 8 * PACK], F32, name="late", offset=19 * 1024)
         board_sb = late[:, 0:NP]
         gain_sb = [late[:, NP + 8 * t : NP + 8 * t + 1] for t in range(PACK)]
         with nc.allow_non_contiguous_dma(reason="one gain value a partition"):
@@ -154,6 +174,8 @@ def tile_list_clue_association_scores_kernel(
                 out=w2_codes[:].bitcast(I32).rearrange("p a (t g j) -> p a t g j", t=PACK, j=2),
                 in_=w2_raw[:].rearrange("p a (g t j) -> p a t g j", t=PACK, j=2),
             )
+
+        def deal_w2_scales():
             for q in range(4):
                 rows = slice(32 * q, 32 * q + 4)
                 nc.vector.tensor_copy(
@@ -182,7 +204,7 @@ def tile_list_clue_association_scores_kernel(
             return acc
 
         def gated(t, hf, on_vector):
-            a_ps = product("w1", t, hf, 3)
+            a_ps = product("w1", t, hf, BUF_A)
             turns_u = ring.tile([P, BANK], U32, name="turns_u")
             nc.scalar.activation(out=turns_u[:], in_=a_ps[:], func=ACT.Copy, scale=1.0 / TWO_PI, bias=ROUND)
             turns = ring.tile([P, BANK], F32, name="turns")
@@ -198,33 +220,44 @@ def tile_list_clue_association_scores_kernel(
             )
             sine = ring.tile([P, BANK], F32, name="sine")
             nc.scalar.activation(out=sine[:], in_=angle[:], func=ACT.Sin)
-            b_ps = product("w2", t, hf, 2)
+            b_ps = product("w2", t, hf, BUF_B)
             prod = ring.tile([P, BANK], F32, name="prod", bufs=6)
             nc.vector.tensor_tensor(out=prod[:], in0=b_ps[:], in1=sine[:], op=ALU.mult)
             return prod
 
         def finish_h(t, hf, prod):
-            d_ps = product("w3", t, hf, 3)
-            nc.vector.tensor_tensor(out=h_sb[t][:, hf * BANK : (hf + 1) * BANK], in0=d_ps[:], in1=prod[:], op=ALU.add)
+            d_ps = product("w3", t, hf, BUF_D)
+            if (t, hf) in G_ADD:
+                d_sb = ring.tile([P, BANK], F32, name="d_sb", bufs=3)
+                nc.scalar.copy(out=d_sb[:], in_=d_ps[:])
+                nc.gpsimd.tensor_tensor(out=h_sb[t][:, hf * BANK : (hf + 1) * BANK], in0=d_sb[:], in1=prod[:], op=ALU.add)
+            else:
+                nc.vector.tensor_tensor(out=h_sb[t][:, hf * BANK : (hf + 1) * BANK], in0=d_ps[:], in1=prod[:], op=ALU.add)
 
         def pick(t):
             picked = ring.tile([P, NP], F32, name="picked", bufs=2)
             nc.vector.tensor_copy(picked[:], h_sb[t][:].indirect(pos2_sb[:]))
             nc.vector.tensor_copy(x1_rows[:, t, :], h_sb[t][:].indirect(pos1_sb[:]))
-            mag = ring.tile([P, NP], F32, name="mag", tag="mag", bufs=1, align_bytes=64)
+            mag = ring.tile([P, NP], F32, name="mag", bufs=2)
             nc.scalar.activation(out=mag[:], in_=picked[:], func=ACT.Abs)
-            nc.scalar.activation(out=x2_rows[:, t, :], in_=mag[:], func=ACT.Copy, scale=gain_sb[t])
+            x2_row = x2_bf[:].rearrange("p (c t) -> p t c", t=PACK)[:, t, :]
+            if t < 2:
+                nc.scalar.activation(out=x2_row, in_=mag[:], func=ACT.Copy, scale=gain_sb[t])
+            else:
+                nc.vector.tensor_scalar(out=x2_row, in0=mag[:], scalar1=gain_sb[t], scalar2=None, op0=ALU.mult)
 
         units = [(0, 0), (1, 0), (0, 1), (1, 1), (2, 0), (2, 1), (3, 0), (3, 1)]
         LAG = 4
         prods = {}
         for i in range(len(units) + LAG):
             if i == 0:
+                deal_w2_scales()
                 deal_w2()
             if i < len(units):
                 prods[i] = gated(*units[i], i < V_TURNS)
             if i == 1:
-                prepare_w("w3", 0, 0, PACK, "vector")
+                for t in range(0, PACK, W3A_STEP):
+                    prepare_w("w3", 0, t, t + W3A_STEP, W3A_ENGINE)
             if 2 <= i < 2 + PACK:
                 prepare_w("w3", 1, i - 2, i - 1, W3_ENGINE)
             if i >= LAG:
@@ -233,12 +266,8 @@ def tile_list_clue_association_scores_kernel(
                 if hf == HALVES - 1:
                     pick(t)
 
-        nc.vector.tensor_copy(
-            out=x2_bf[:].rearrange("p (c i t) -> p c t i", i=4, t=PACK),
-            in_=x2_rows[:].rearrange("p t (c i) -> p c t i", i=4),
-        )
         x1_q = []
-        x1_all = ring.tile([P, NP * PACK], BF16, name="x1_all", tag="mag", bufs=1, align_bytes=64)
+        x1_all = ring.tile([P, NP * PACK], BF16, name="x1_all", bufs=1, align_bytes=64)
         for m in range(NP // P):
             x1_bf = x1_all[:, m * P * PACK : (m + 1) * P * PACK]
             nc.scalar.copy(
@@ -254,7 +283,7 @@ def tile_list_clue_association_scores_kernel(
             nc.vector.quantize_mx(out=x1_codes[:].bitcast(FP8X4), scales=x1_scale[:], in_=x1_q[m])
             x1_mx.append((x1_codes, x1_scale))
         for m in range(NP // P):
-            e_ps = psum.tile([P, BANK], F32, name="acc_w1", tag="acc_w1", bufs=3)
+            e_ps = psum.tile([P, BANK], F32, name="acc_w1", tag="acc_w1", bufs=BUF_A)
             nc.tensor.matmul_mx(
                 out=e_ps[:],
                 lhsT=x1_mx[m][0][:].bitcast(FP8X4),

@@ -25,12 +25,12 @@ BANK = 512
 HALVES = S // BANK
 ROUND = 1.5 * 2.0**23
 TWO_PI = 2.0 * math.pi
-W3_ENGINE = "gpsimd"
 V_TURNS = 0
-W3A_ENGINE = "vector"
-WARM = False
-W3A_STEP = 4
-G_ADD = ((1, 0), (2, 0), (3, 0))
+LEAD = ("unit1", "unit3", "unit5", "unit6")
+W1B_PLAN = ((0, 1, "vector", "bf1"), (1, 4, "vector", "bf1"))
+W3_PLAN = ((2, 0, "vector"), (3, 1, "scalar"), (5, 2, "scalar"), (7, 3, "scalar"))
+WARM = True
+G_ADD = ()
 BUF_A, BUF_B, BUF_D = 3, 2, 3
 
 
@@ -55,14 +55,15 @@ def tile_list_clue_association_scores_kernel(
         v_scale = [held([P, S], U8, f"v_scale{a}") for a in range(PASSES)]
         v_codes = [[held([P, BANK], U32, f"v_codes{a}_{hf}") for hf in range(HALVES)] for a in range(PASSES)]
         w_raw = {}
-        pairs = [(n, a) for n in ("w1", "w3") for a in range(PASSES)]
-        w_bf = {(n, a): held([P, H * PACK], BF16, f"{n}_bf{a}") for n, a in pairs}
-        w_codes = {(n, a): held([P, H], U32, f"{n}_codes{a}") for n, a in pairs}
-        w_scale = {(n, a): held([P, H], U8, f"{n}_scale{a}") for n, a in pairs}
+        w1_codes = [held([P, H], U32, f"w1_codes{a}") for a in range(PASSES)]
+        w1_scale = [held([P, H], U8, f"w1_scale{a}") for a in range(PASSES)]
+        w3_codes = [held([P, PASSES * P], U32, f"w3_codes{t}") for t in range(PACK)]
+        w3_scale = [held([P, PASSES * P], U8, f"w3_scale{t}") for t in range(PACK)]
         w2_codes = held([P, PASSES, 2 * H], U8, "w2_codes")
         w2_scale = held([P, PASSES, H], U8, "w2_scale")
-        h_sb = [held([P, S], F32, f"h_sb{t}") for t in range(PACK)]
+        h_sb = {}
         x1_rows = held([P, PACK, NP], BF16, "x1_rows")
+        x2_rows = held([P, PACK - 1, NP], BF16, "x2_rows", tag="x2_rows")
         x2_bf = held([P, NP * PACK], BF16, "x2_bf")
         x2_codes = held([P, NP], U32, "x2_codes")
         x2_scale = held([P, NP], U8, "x2_scale")
@@ -78,8 +79,12 @@ def tile_list_clue_association_scores_kernel(
             nc.gpsimd.memset(v_scale[a][:].bitcast(I32), 0)
         nc.sync.dma_start(offs_sb[:], offs)
         nc.sync.dma_start(out=tsc_sb[0:32, :].bitcast(I32), in_=tab_scales.rearrange("a q t -> (a q) t").bitcast(I32))
-        nc.sync.dma_start(pos1_sb[:], pos1)
-        nc.sync.dma_start(pos2_sb[:], pos2)
+        w2_sc_raw = held([P, PASSES, H // 4], I32, "w2_sc_raw")
+        for q in range(4):
+            nc.sync.dma_start(
+                out=w2_sc_raw[32 * q : 32 * q + 4, :, :],
+                in_=w2_scales.bitcast(I32)[:, 4 * q : 4 * q + 4, :].rearrange("a r c -> r a c"),
+            )
         w_dram = {"w1": w1, "w3": w3}
 
         def load_w(n, a):
@@ -100,23 +105,19 @@ def tile_list_clue_association_scores_kernel(
         load_table(0)
         w_raw["w1", 0] = held([P, PACK, H], F32, "w1_raw0")[:]
         load_w("w1", 0)
+        nc.sync.dma_start(pos1_sb[:], pos1)
+        nc.sync.dma_start(pos2_sb[:], pos2)
 
         nc.vector.tensor_copy(tsc_pick[:], tsc_sb[:].indirect(offs_sb[:]))
         moves = [(a, q) for a in range(PASSES) for q in range(4)]
-        for a, q in moves[:6]:
+        for a, q in moves[:4]:
+            move_scale_rows(a, q)
+        tab_sb[1] = reuse.tile([P, T], U32, name="tab_sb1", offset=0)
+        load_table(1)
+        for a, q in moves[4:]:
             move_scale_rows(a, q)
         w_raw["w1", 1] = reuse.tile([P, PACK, H], F32, name="w1_raw1", offset=19 * 1024)[:]
         load_w("w1", 1)
-        for a, q in moves[6:]:
-            move_scale_rows(a, q)
-        w2_sc_raw = reuse.tile([P, PASSES, H // 4], I32, name="w2_sc_raw", offset=16 * 1024)
-        for q in range(4):
-            nc.sync.dma_start(
-                out=w2_sc_raw[32 * q : 32 * q + 4, :, :],
-                in_=w2_scales.bitcast(I32)[:, 4 * q : 4 * q + 4, :].rearrange("a r c -> r a c"),
-            )
-        tab_sb[1] = reuse.tile([P, T], U32, name="tab_sb1", offset=0)
-        load_table(1)
         w2_raw = reuse.tile([P, PASSES, H // 2], I32, name="w2_raw", offset=17 * 1024)
         nc.sync.dma_start(out=w2_raw[:], in_=w2_words.bitcast(I32).rearrange("a p c -> p a c"))
 
@@ -125,49 +126,28 @@ def tile_list_clue_association_scores_kernel(
                 cols = BANK // 16
                 nc.vector.tensor_copy(v_codes[a][hf][:], tab_sb[a][:].indirect(offs_sb[:, hf * cols : (hf + 1) * cols]))
 
-        def round_w(n, a, t0, t1, engine):
-            dst = w_bf[n, a][:].rearrange("p (t g j i) -> p t g i j", t=PACK, j=4, i=PACK)[:, t0:t1]
+        def round_w(dst, n, a, t0, t1, engine):
+            dst = dst.rearrange("p (t g j i) -> p t g i j", t=t1 - t0, j=4, i=PACK)
             src = w_raw[n, a].rearrange("p i (g t j) -> p t g i j", t=PACK, j=4)[:, t0:t1]
             if engine == "scalar":
                 nc.scalar.copy(out=dst, in_=src)
-            elif engine == "vector":
-                nc.vector.tensor_copy(out=dst, in_=src)
             else:
-                nc.gpsimd.tensor_scalar(
-                    out=dst.rearrange("p t g i j -> p t g j i"),
-                    in0=src.rearrange("p t g i j -> p t g j i"),
-                    scalar1=1.0,
-                    scalar2=0.0,
-                    op0=ALU.mult,
-                    op1=ALU.add,
-                )
+                nc.vector.tensor_copy(out=dst, in_=src)
 
-        def quantize_w(n, a, t0, t1):
+        def prepare_w1(a, t0, t1, engine, tag):
+            rounded = held([P, (t1 - t0) * P * PACK], BF16, f"w1_bf{a}_{t0}", tag=tag)
+            round_w(rounded[:], "w1", a, t0, t1, engine)
             nc.vector.quantize_mx(
-                out=w_codes[n, a][:, P * t0 : P * t1].bitcast(FP8X4),
-                scales=w_scale[n, a][:, P * t0 : P * t1],
-                in_=w_bf[n, a][:, P * PACK * t0 : P * PACK * t1],
+                out=w1_codes[a][:, P * t0 : P * t1].bitcast(FP8X4),
+                scales=w1_scale[a][:, P * t0 : P * t1],
+                in_=rounded[:],
             )
 
-        def prepare_w(n, a, t0, t1, engine):
-            round_w(n, a, t0, t1, engine)
-            quantize_w(n, a, t0, t1)
-
-        gather_table(0)
-        for a in range(PASSES):
-            prepare_w("w1", a, 0, PACK, "scalar")
-        gather_table(1)
-
-        for a in range(PASSES):
-            w_raw["w3", a] = reuse.tile([P, PACK, H], F32, name=f"w3_raw{a}", offset=28 * 1024 + a * PACK * H * 4)[:]
-            load_w("w3", a)
-        late = reuse.tile([P, NP + 8 * PACK], F32, name="late", offset=19 * 1024)
-        board_sb = late[:, 0:NP]
-        gain_sb = [late[:, NP + 8 * t : NP + 8 * t + 1] for t in range(PACK)]
-        with nc.allow_non_contiguous_dma(reason="one gain value a partition"):
-            for t in range(PACK):
-                nc.sync.dma_start(out=gain_sb[t], in_=gain.rearrange("(g t j) -> t g j", t=PACK, j=4)[t])
-        nc.sync.dma_start(out=board_sb, in_=board.partition_broadcast(P))
+        def prepare_w3(t, engine):
+            rounded = [held([P, PASSES * P * PACK], BF16, f"w3_bf{t}")][0]
+            for a in range(PASSES):
+                round_w(rounded[:, a * P * PACK : (a + 1) * P * PACK], "w3", a, t, t + 1, engine)
+            nc.vector.quantize_mx(out=w3_codes[t][:].bitcast(FP8X4), scales=w3_scale[t][:], in_=rounded[:])
 
         def deal_w2():
             nc.vector.tensor_copy(
@@ -183,15 +163,36 @@ def tile_list_clue_association_scores_kernel(
                     in_=w2_sc_raw[rows].rearrange("p a (g t) -> p a t g", t=PACK),
                 )
 
+        deal_w2_scales()
+        gather_table(0)
+        prepare_w1(0, 0, PACK, "scalar", "bf0")
+        gather_table(1)
+        for t0, t1, engine, tag in W1B_PLAN:
+            prepare_w1(1, t0, t1, engine, tag)
+
+        for a in range(PASSES):
+            w_raw["w3", a] = reuse.tile([P, PACK, H], F32, name=f"w3_raw{a}", offset=28 * 1024 + a * PACK * H * 4)[:]
+            load_w("w3", a)
+        late = reuse.tile([P, NP + 8 * PACK], F32, name="late", offset=19 * 1024)
+        board_sb = late[:, 0:NP]
+        gain_sb = [late[:, NP + 8 * t : NP + 8 * t + 1] for t in range(PACK)]
+        with nc.allow_non_contiguous_dma(reason="one gain value a partition"):
+            for t in range(PACK):
+                nc.sync.dma_start(out=gain_sb[t], in_=gain.rearrange("(g t j) -> t g j", t=PACK, j=4)[t])
+        nc.sync.dma_start(out=board_sb, in_=board.partition_broadcast(P))
+
         def product(n, t, hf, bufs):
             acc = psum.tile([P, BANK], F32, name=f"acc_{n}", tag=f"acc_{n}", bufs=bufs)
             for a in range(PASSES):
                 if n == "w2":
                     lhsT = w2_codes[:, a, 2 * P * t : 2 * P * (t + 1)].bitcast(FP4X4)
                     lhsT_scale = w2_scale[:, a, P * t : P * (t + 1)]
+                elif n == "w1":
+                    lhsT = w1_codes[a][:, P * t : P * (t + 1)].bitcast(FP8X4)
+                    lhsT_scale = w1_scale[a][:, P * t : P * (t + 1)]
                 else:
-                    lhsT = w_codes[n, a][:, P * t : P * (t + 1)].bitcast(FP8X4)
-                    lhsT_scale = w_scale[n, a][:, P * t : P * (t + 1)]
+                    lhsT = w3_codes[t][:, P * a : P * (a + 1)].bitcast(FP8X4)
+                    lhsT_scale = w3_scale[t][:, P * a : P * (a + 1)]
                 nc.tensor.matmul_mx(
                     out=acc[:],
                     lhsT=lhsT,
@@ -207,7 +208,7 @@ def tile_list_clue_association_scores_kernel(
             a_ps = product("w1", t, hf, BUF_A)
             turns_u = ring.tile([P, BANK], U32, name="turns_u")
             nc.scalar.activation(out=turns_u[:], in_=a_ps[:], func=ACT.Copy, scale=1.0 / TWO_PI, bias=ROUND)
-            turns = ring.tile([P, BANK], F32, name="turns")
+            turns = held([P, BANK], F32, "turns", tag=f"unit{HALVES * t + hf}")
             if on_vector:
                 nc.vector.tensor_scalar(
                     out=turns[:], in0=turns_u[:].bitcast(I32), scalar1=-ROUND, scalar2=None, op0=ALU.add
@@ -227,6 +228,8 @@ def tile_list_clue_association_scores_kernel(
 
         def finish_h(t, hf, prod):
             d_ps = product("w3", t, hf, BUF_D)
+            if hf == 0:
+                h_sb[t] = held([P, S], F32, f"h_sb{t}", tag=LEAD[t])
             if (t, hf) in G_ADD:
                 d_sb = ring.tile([P, BANK], F32, name="d_sb", bufs=3)
                 nc.scalar.copy(out=d_sb[:], in_=d_ps[:])
@@ -235,31 +238,39 @@ def tile_list_clue_association_scores_kernel(
                 nc.vector.tensor_tensor(out=h_sb[t][:, hf * BANK : (hf + 1) * BANK], in0=d_ps[:], in1=prod[:], op=ALU.add)
 
         def pick(t):
-            picked = ring.tile([P, NP], F32, name="picked", bufs=2)
+            if t < PACK - 1:
+                picked = ring.tile([P, NP], F32, name="picked", bufs=2)
+            else:
+                picked = held([P, NP], F32, "picked_last", tag="last")
             nc.vector.tensor_copy(picked[:], h_sb[t][:].indirect(pos2_sb[:]))
             nc.vector.tensor_copy(x1_rows[:, t, :], h_sb[t][:].indirect(pos1_sb[:]))
-            mag = ring.tile([P, NP], F32, name="mag", bufs=2)
-            nc.scalar.activation(out=mag[:], in_=picked[:], func=ACT.Abs)
-            x2_row = x2_bf[:].rearrange("p (c t) -> p t c", t=PACK)[:, t, :]
-            if t < 2:
-                nc.scalar.activation(out=x2_row, in_=mag[:], func=ACT.Copy, scale=gain_sb[t])
+            if t < PACK - 1:
+                mag = ring.tile([P, NP], F32, name="mag", bufs=2)
             else:
-                nc.vector.tensor_scalar(out=x2_row, in0=mag[:], scalar1=gain_sb[t], scalar2=None, op0=ALU.mult)
+                mag = held([P, NP], F32, "mag_last", tag="x2_rows")
+            nc.scalar.activation(out=mag[:], in_=picked[:], func=ACT.Abs)
+            if t < PACK - 1:
+                nc.scalar.activation(out=x2_rows[:, t, :], in_=mag[:], func=ACT.Copy, scale=gain_sb[t])
+            else:
+                x2_last = x2_bf[:].rearrange("p (c t) -> p t c", t=PACK)[:, t, :]
+                nc.vector.tensor_scalar(out=x2_last, in0=mag[:], scalar1=gain_sb[t], scalar2=None, op0=ALU.mult)
+            if t == PACK - 2:
+                nc.scalar.copy(
+                    out=x2_bf[:].rearrange("p (c i t) -> p c t i", i=4, t=PACK)[:, :, 0 : PACK - 1, :],
+                    in_=x2_rows[:].rearrange("p t (c i) -> p c t i", i=4),
+                )
 
-        units = [(0, 0), (1, 0), (0, 1), (1, 1), (2, 0), (2, 1), (3, 0), (3, 1)]
+        units = [(t, hf) for t in range(PACK) for hf in range(HALVES)]
         LAG = 4
         prods = {}
         for i in range(len(units) + LAG):
             if i == 0:
-                deal_w2_scales()
                 deal_w2()
             if i < len(units):
                 prods[i] = gated(*units[i], i < V_TURNS)
-            if i == 1:
-                for t in range(0, PACK, W3A_STEP):
-                    prepare_w("w3", 0, t, t + W3A_STEP, W3A_ENGINE)
-            if 2 <= i < 2 + PACK:
-                prepare_w("w3", 1, i - 2, i - 1, W3_ENGINE)
+            for step, t, engine in W3_PLAN:
+                if step == i:
+                    prepare_w3(t, engine)
             if i >= LAG:
                 t, hf = units[i - LAG]
                 finish_h(t, hf, prods[i - LAG])
@@ -267,7 +278,7 @@ def tile_list_clue_association_scores_kernel(
                     pick(t)
 
         x1_q = []
-        x1_all = ring.tile([P, NP * PACK], BF16, name="x1_all", bufs=1, align_bytes=64)
+        x1_all = held([P, NP * PACK], BF16, "x1_all", tag="last")
         for m in range(NP // P):
             x1_bf = x1_all[:, m * P * PACK : (m + 1) * P * PACK]
             nc.scalar.copy(

@@ -28,9 +28,9 @@ TWO_PI = 2.0 * math.pi
 V_TURNS = 0
 LEAD = ("unit1", "unit3", "unit5", "unit6")
 W1B_PLAN = ((0, 1, "vector", "bf1"), (1, 4, "vector", "bf1"))
-W3_PLAN = ((2, 0, "vector"), (3, 1, "scalar"), (5, 2, "scalar"), (7, 3, "scalar"))
+W3_PLAN = ((2, 0, "vector"), (3, 1, "gpsimd"), (4, 2, "gpsimd"), (5, 3, "gpsimd"))
 WARM = True
-G_ADD = ()
+G_ADD = ((1, 0), (2, 0), (3, 0))
 BUF_A, BUF_B, BUF_D = 3, 2, 3
 
 
@@ -131,8 +131,17 @@ def tile_list_clue_association_scores_kernel(
             src = w_raw[n, a].rearrange("p i (g t j) -> p t g i j", t=PACK, j=4)[:, t0:t1]
             if engine == "scalar":
                 nc.scalar.copy(out=dst, in_=src)
-            else:
+            elif engine == "vector":
                 nc.vector.tensor_copy(out=dst, in_=src)
+            else:
+                nc.gpsimd.tensor_scalar(
+                    out=dst.rearrange("p t g i j -> p g t j i"),
+                    in0=src.rearrange("p t g i j -> p g t j i"),
+                    scalar1=1.0,
+                    scalar2=0.0,
+                    op0=ALU.mult,
+                    op1=ALU.add,
+                )
 
         def prepare_w1(a, t0, t1, engine, tag):
             rounded = held([P, (t1 - t0) * P * PACK], BF16, f"w1_bf{a}_{t0}", tag=tag)
@@ -277,35 +286,43 @@ def tile_list_clue_association_scores_kernel(
                 if hf == HALVES - 1:
                     pick(t)
 
-        x1_q = []
-        x1_all = held([P, NP * PACK], BF16, "x1_all", tag="last")
-        for m in range(NP // P):
-            x1_bf = x1_all[:, m * P * PACK : (m + 1) * P * PACK]
+        x1_bf = held([P, NP * PACK], BF16, "x1_bf", tag="last")
+        x1_codes = held([P, NP], U32, "x1_codes")
+        x1_scale = held([P, NP], U8, "x1_scale")
+        tiles = NP // P
+        for m in range(tiles):
             nc.scalar.copy(
-                out=x1_bf.rearrange("p (c i t) -> p c t i", i=4, t=PACK),
+                out=x1_bf[:, m * P * PACK : (m + 1) * P * PACK].rearrange("p (c i t) -> p c t i", i=4, t=PACK),
                 in_=x1_rows[:, :, m * P : (m + 1) * P].rearrange("p t (c i) -> p c t i", i=4),
             )
-            x1_q.append(x1_bf)
+
+        def quantize_x1(m0, m1):
+            nc.vector.quantize_mx(
+                out=x1_codes[:, m0 * P : m1 * P].bitcast(FP8X4),
+                scales=x1_scale[:, m0 * P : m1 * P],
+                in_=x1_bf[:, m0 * P * PACK : m1 * P * PACK],
+            )
+
+        quantize_x1(0, 1)
         nc.vector.quantize_mx(out=x2_codes[:].bitcast(FP8X4), scales=x2_scale[:], in_=x2_bf[:])
-        x1_mx = []
-        for m in range(NP // P):
-            x1_codes = ring.tile([P, P], U32, name="x1_codes", bufs=4, align_bytes=64)
-            x1_scale = ring.tile([P, P], U8, name="x1_scale", bufs=4, align_bytes=64)
-            nc.vector.quantize_mx(out=x1_codes[:].bitcast(FP8X4), scales=x1_scale[:], in_=x1_q[m])
-            x1_mx.append((x1_codes, x1_scale))
-        for m in range(NP // P):
+        quantize_x1(1, 2)
+        quantize_x1(2, tiles)
+        for m in range(tiles):
             e_ps = psum.tile([P, BANK], F32, name="acc_w1", tag="acc_w1", bufs=BUF_A)
             nc.tensor.matmul_mx(
                 out=e_ps[:],
-                lhsT=x1_mx[m][0][:].bitcast(FP8X4),
-                lhsT_scale=x1_mx[m][1][:],
+                lhsT=x1_codes[:, m * P : (m + 1) * P].bitcast(FP8X4),
+                lhsT_scale=x1_scale[:, m * P : (m + 1) * P],
                 rhs=x2_codes[:].bitcast(FP8X4),
                 rhs_scale=x2_scale[:],
                 start=True,
                 stop=True,
             )
             shifted = ring.tile([P, NP], F32, name="shifted", bufs=4)
-            nc.vector.tensor_tensor(out=shifted[:], in0=e_ps[:], in1=board_sb, op=ALU.add)
             score = ring.tile([P, NP], F32, name="score", bufs=4)
-            nc.scalar.activation(out=score[:], in_=shifted[:], func=ACT.Tanh)
-            nc.sync.dma_start(out=out[m * P : (m + 1) * P, :], in_=score[:])
+            width = NP if m < tiles - 1 else NP // 2
+            for c0 in range(0, NP, width):
+                cols = slice(c0, c0 + width)
+                nc.vector.tensor_tensor(out=shifted[:, cols], in0=e_ps[:, cols], in1=board_sb[:, cols], op=ALU.add)
+                nc.scalar.activation(out=score[:, cols], in_=shifted[:, cols], func=ACT.Tanh)
+                nc.sync.dma_start(out=out[m * P : (m + 1) * P, cols], in_=score[:, cols])

import math
from contextlib import ExitStack

import concourse.mybir as mybir

K, H, T, S, NP = 1024, 512, 4096, 1024, 512
FLOPS = 3 * 2 * K * H * S + 2 * H * NP * NP

F32 = mybir.dt.float32
BF16 = mybir.dt.bfloat16
I32 = mybir.dt.int32
U32 = mybir.dt.uint32
U16 = mybir.dt.uint16
U8 = mybir.dt.uint8
FP8X4 = mybir.dt.float8_e4m3fn_x4
FP4X4 = mybir.dt.float4_e2m1fn_x4
ACT = mybir.ActivationFunctionType
ALU = mybir.AluOpType

P = 128
PACK = 4
K_PASS = P * PACK
PASSES = K // K_PASS
BANK = 512
HALVES = S // BANK
ROUND = 1.5 * 2.0**23
TWO_PI = 2.0 * math.pi
V_TURNS = 0
LEAD = ("unit1", "unit3", "unit5", "unit6")
W1B_PLAN = ((0, 1, "vector", "bf1"), (1, 4, "vector", "bf1"))
W3_PLAN = ((2, 0, "vector"), (3, 1, "gpsimd"), (4, 2, "gpsimd"), (5, 3, "gpsimd"))
WARM = True
G_ADD = ((1, 0), (2, 0), (3, 0))
BUF_A, BUF_B, BUF_D = 3, 2, 3


def tile_list_clue_association_scores_kernel(
    tc, tab_words, tab_scales, offs, pos1, pos2, w1, w2_words, w2_scales, w3, gain, board, out
):
    nc = tc.nc
    with ExitStack() as ctx:
        keep = ctx.enter_context(tc.tile_pool(name="keep", bufs=1))
        reuse = ctx.enter_context(tc.tile_pool(name="reuse", bufs=1))
        ring = ctx.enter_context(tc.tile_pool(name="ring", bufs=3))
        psum = ctx.enter_context(tc.psum_pool(name="psum", bufs=1))

        def held(shape, dtype, name, tag=""):
            return keep.tile(shape, dtype, name=name, tag=tag, align_bytes=64)

        offs_sb = held([P, S // 16], U16, "offs_sb")
        pos1_sb = held([P, NP // 16], U16, "pos1_sb")
        pos2_sb = held([P, NP // 16], U16, "pos2_sb")
        tsc_sb = reuse.tile([P, T], U8, name="tsc_sb", offset=15 * 1024 + 64)
        tsc_pick = held([P, S], U8, "tsc_pick")
        v_scale = [held([P, S], U8, f"v_scale{a}") for a in range(PASSES)]
        v_codes = [[held([P, BANK], U32, f"v_codes{a}_{hf}") for hf in range(HALVES)] for a in range(PASSES)]
        w_raw = {}
        w1_codes = [held([P, H], U32, f"w1_codes{a}") for a in range(PASSES)]
        w1_scale = [held([P, H], U8, f"w1_scale{a}") for a in range(PASSES)]
        w3_codes = [held([P, PASSES * P], U32, f"w3_codes{t}") for t in range(PACK)]
        w3_scale = [held([P, PASSES * P], U8, f"w3_scale{t}") for t in range(PACK)]
        w2_codes = held([P, PASSES, 2 * H], U8, "w2_codes")
        w2_scale = held([P, PASSES, H], U8, "w2_scale")
        h_sb = {}
        x1_rows = held([P, PACK, NP], BF16, "x1_rows")
        x2_rows = held([P, PACK - 1, NP], BF16, "x2_rows", tag="x2_rows")
        x2_bf = held([P, NP * PACK], BF16, "x2_bf")
        x2_codes = held([P, NP], U32, "x2_codes")
        x2_scale = held([P, NP], U8, "x2_scale")

        if WARM:
            warm = held([P, 16], F32, "warm")
            nc.gpsimd.memset(warm[:, 0:1], 0.0)
            nc.scalar.activation(out=warm[:, 8:9], in_=warm[:, 0:1], func=ACT.Silu)
        nc.vector.memset(tsc_sb[32:64, :].bitcast(I32), 0)
        nc.vector.memset(tsc_sb[64:P, :].bitcast(I32), 0)
        nc.gpsimd.memset(w2_scale[:].bitcast(I32), 0)
        for a in range(PASSES):
            nc.gpsimd.memset(v_scale[a][:].bitcast(I32), 0)
        nc.sync.dma_start(offs_sb[:], offs)
        nc.sync.dma_start(out=tsc_sb[0:32, :].bitcast(I32), in_=tab_scales.rearrange("a q t -> (a q) t").bitcast(I32))
        w2_sc_raw = held([P, PASSES, H // 4], I32, "w2_sc_raw")
        for q in range(4):
            nc.sync.dma_start(
                out=w2_sc_raw[32 * q : 32 * q + 4, :, :],
                in_=w2_scales.bitcast(I32)[:, 4 * q : 4 * q + 4, :].rearrange("a r c -> r a c"),
            )
        w_dram = {"w1": w1, "w3": w3}

        def load_w(n, a):
            rows = w_dram[n][a * K_PASS : (a + 1) * K_PASS, :]
            nc.sync.dma_start(out=w_raw[n, a], in_=rows.rearrange("(p i) c -> p i c", i=PACK))

        def load_table(a):
            nc.sync.dma_start(out=tab_sb[a][:].bitcast(I32), in_=tab_words[a].rearrange("p n i -> p (n i)").bitcast(I32))

        def move_scale_rows(a, q):
            first = 16 * a + 4 * q
            nc.sync.dma_start(
                out=v_scale[a][32 * q : 32 * q + 4, :].bitcast(I32),
                in_=tsc_pick[first : first + 4, :].bitcast(I32),
            )

        tab_sb = {0: reuse.tile([P, T], U32, name="tab_sb0", offset=28 * 1024)}
        load_table(0)
        w_raw["w1", 0] = held([P, PACK, H], F32, "w1_raw0")[:]
        load_w("w1", 0)
        nc.sync.dma_start(pos1_sb[:], pos1)
        nc.sync.dma_start(pos2_sb[:], pos2)

        nc.vector.tensor_copy(tsc_pick[:], tsc_sb[:].indirect(offs_sb[:]))
        moves = [(a, q) for a in range(PASSES) for q in range(4)]
        for a, q in moves[:4]:
            move_scale_rows(a, q)
        tab_sb[1] = reuse.tile([P, T], U32, name="tab_sb1", offset=0)
        load_table(1)
        for a, q in moves[4:]:
            move_scale_rows(a, q)
        w_raw["w1", 1] = reuse.tile([P, PACK, H], F32, name="w1_raw1", offset=19 * 1024)[:]
        load_w("w1", 1)
        w2_raw = reuse.tile([P, PASSES, H // 2], I32, name="w2_raw", offset=17 * 1024)
        nc.sync.dma_start(out=w2_raw[:], in_=w2_words.bitcast(I32).rearrange("a p c -> p a c"))

        def gather_table(a):
            for hf in range(HALVES):
                cols = BANK // 16
                nc.vector.tensor_copy(v_codes[a][hf][:], tab_sb[a][:].indirect(offs_sb[:, hf * cols : (hf + 1) * cols]))

        def round_w(dst, n, a, t0, t1, engine):
            dst = dst.rearrange("p (t g j i) -> p t g i j", t=t1 - t0, j=4, i=PACK)
            src = w_raw[n, a].rearrange("p i (g t j) -> p t g i j", t=PACK, j=4)[:, t0:t1]
            if engine == "scalar":
                nc.scalar.copy(out=dst, in_=src)
            elif engine == "vector":
                nc.vector.tensor_copy(out=dst, in_=src)
            else:
                nc.gpsimd.tensor_scalar(
                    out=dst.rearrange("p t g i j -> p g t j i"),
                    in0=src.rearrange("p t g i j -> p g t j i"),
                    scalar1=1.0,
                    scalar2=0.0,
                    op0=ALU.mult,
                    op1=ALU.add,
                )

        def prepare_w1(a, t0, t1, engine, tag):
            rounded = held([P, (t1 - t0) * P * PACK], BF16, f"w1_bf{a}_{t0}", tag=tag)
            round_w(rounded[:], "w1", a, t0, t1, engine)
            nc.vector.quantize_mx(
                out=w1_codes[a][:, P * t0 : P * t1].bitcast(FP8X4),
                scales=w1_scale[a][:, P * t0 : P * t1],
                in_=rounded[:],
            )

        def prepare_w3(t, engine):
            rounded = [held([P, PASSES * P * PACK], BF16, f"w3_bf{t}")][0]
            for a in range(PASSES):
                round_w(rounded[:, a * P * PACK : (a + 1) * P * PACK], "w3", a, t, t + 1, engine)
            nc.vector.quantize_mx(out=w3_codes[t][:].bitcast(FP8X4), scales=w3_scale[t][:], in_=rounded[:])

        def deal_w2():
            nc.vector.tensor_copy(
                out=w2_codes[:].bitcast(I32).rearrange("p a (t g j) -> p a t g j", t=PACK, j=2),
                in_=w2_raw[:].rearrange("p a (g t j) -> p a t g j", t=PACK, j=2),
            )

        def deal_w2_scales():
            for q in range(4):
                rows = slice(32 * q, 32 * q + 4)
                nc.vector.tensor_copy(
                    out=w2_scale[rows].bitcast(I32).rearrange("p a (t g) -> p a t g", t=PACK),
                    in_=w2_sc_raw[rows].rearrange("p a (g t) -> p a t g", t=PACK),
                )

        deal_w2_scales()
        gather_table(0)
        prepare_w1(0, 0, PACK, "scalar", "bf0")
        gather_table(1)
        for t0, t1, engine, tag in W1B_PLAN:
            prepare_w1(1, t0, t1, engine, tag)

        for a in range(PASSES):
            w_raw["w3", a] = reuse.tile([P, PACK, H], F32, name=f"w3_raw{a}", offset=28 * 1024 + a * PACK * H * 4)[:]
            load_w("w3", a)
        late = reuse.tile([P, NP + 8 * PACK], F32, name="late", offset=19 * 1024)
        board_sb = late[:, 0:NP]
        gain_sb = [late[:, NP + 8 * t : NP + 8 * t + 1] for t in range(PACK)]
        with nc.allow_non_contiguous_dma(reason="one gain value a partition"):
            for t in range(PACK):
                nc.sync.dma_start(out=gain_sb[t], in_=gain.rearrange("(g t j) -> t g j", t=PACK, j=4)[t])
        nc.sync.dma_start(out=board_sb, in_=board.partition_broadcast(P))

        def product(n, t, hf, bufs):
            acc = psum.tile([P, BANK], F32, name=f"acc_{n}", tag=f"acc_{n}", bufs=bufs)
            for a in range(PASSES):
                if n == "w2":
                    lhsT = w2_codes[:, a, 2 * P * t : 2 * P * (t + 1)].bitcast(FP4X4)
                    lhsT_scale = w2_scale[:, a, P * t : P * (t + 1)]
                elif n == "w1":
                    lhsT = w1_codes[a][:, P * t : P * (t + 1)].bitcast(FP8X4)
                    lhsT_scale = w1_scale[a][:, P * t : P * (t + 1)]
                else:
                    lhsT = w3_codes[t][:, P * a : P * (a + 1)].bitcast(FP8X4)
                    lhsT_scale = w3_scale[t][:, P * a : P * (a + 1)]
                nc.tensor.matmul_mx(
                    out=acc[:],
                    lhsT=lhsT,
                    lhsT_scale=lhsT_scale,
                    rhs=v_codes[a][hf][:].bitcast(FP8X4),
                    rhs_scale=v_scale[a][:, hf * BANK : (hf + 1) * BANK],
                    start=(a == 0),
                    stop=(a == PASSES - 1),
                )
            return acc

        def gated(t, hf, on_vector):
            a_ps = product("w1", t, hf, BUF_A)
            turns_u = ring.tile([P, BANK], U32, name="turns_u")
            nc.scalar.activation(out=turns_u[:], in_=a_ps[:], func=ACT.Copy, scale=1.0 / TWO_PI, bias=ROUND)
            turns = held([P, BANK], F32, "turns", tag=f"unit{HALVES * t + hf}")
            if on_vector:
                nc.vector.tensor_scalar(
                    out=turns[:], in0=turns_u[:].bitcast(I32), scalar1=-ROUND, scalar2=None, op0=ALU.add
                )
            else:
                nc.scalar.activation(out=turns[:], in_=turns_u[:], func=ACT.Copy, scale=1.0, bias=-ROUND)
            angle = ring.tile([P, BANK], F32, name="angle")
            nc.vector.scalar_tensor_tensor(
                out=angle[:], in0=turns[:], scalar=-TWO_PI, in1=a_ps[:], op0=ALU.mult, op1=ALU.add
            )
            sine = ring.tile([P, BANK], F32, name="sine")
            nc.scalar.activation(out=sine[:], in_=angle[:], func=ACT.Sin)
            b_ps = product("w2", t, hf, BUF_B)
            prod = ring.tile([P, BANK], F32, name="prod", bufs=6)
            nc.vector.tensor_tensor(out=prod[:], in0=b_ps[:], in1=sine[:], op=ALU.mult)
            return prod

        def finish_h(t, hf, prod):
            d_ps = product("w3", t, hf, BUF_D)
            if hf == 0:
                h_sb[t] = held([P, S], F32, f"h_sb{t}", tag=LEAD[t])
            if (t, hf) in G_ADD:
                d_sb = ring.tile([P, BANK], F32, name="d_sb", bufs=3)
                nc.scalar.copy(out=d_sb[:], in_=d_ps[:])
                nc.gpsimd.tensor_tensor(out=h_sb[t][:, hf * BANK : (hf + 1) * BANK], in0=d_sb[:], in1=prod[:], op=ALU.add)
            else:
                nc.vector.tensor_tensor(out=h_sb[t][:, hf * BANK : (hf + 1) * BANK], in0=d_ps[:], in1=prod[:], op=ALU.add)

        def pick(t):
            if t < PACK - 1:
                picked = ring.tile([P, NP], F32, name="picked", bufs=2)
            else:
                picked = held([P, NP], F32, "picked_last", tag="last")
            nc.vector.tensor_copy(picked[:], h_sb[t][:].indirect(pos2_sb[:]))
            nc.vector.tensor_copy(x1_rows[:, t, :], h_sb[t][:].indirect(pos1_sb[:]))
            if t < PACK - 1:
                mag = ring.tile([P, NP], F32, name="mag", bufs=2)
            else:
                mag = held([P, NP], F32, "mag_last", tag="x2_rows")
            nc.scalar.activation(out=mag[:], in_=picked[:], func=ACT.Abs)
            if t < PACK - 1:
                nc.scalar.activation(out=x2_rows[:, t, :], in_=mag[:], func=ACT.Copy, scale=gain_sb[t])
            else:
                x2_last = x2_bf[:].rearrange("p (c t) -> p t c", t=PACK)[:, t, :]
                nc.vector.tensor_scalar(out=x2_last, in0=mag[:], scalar1=gain_sb[t], scalar2=None, op0=ALU.mult)
            if t == PACK - 2:
                nc.scalar.copy(
                    out=x2_bf[:].rearrange("p (c i t) -> p c t i", i=4, t=PACK)[:, :, 0 : PACK - 1, :],
                    in_=x2_rows[:].rearrange("p t (c i) -> p c t i", i=4),
                )

        units = [(t, hf) for t in range(PACK) for hf in range(HALVES)]
        LAG = 4
        prods = {}
        for i in range(len(units) + LAG):
            if i == 0:
                deal_w2()
            if i < len(units):
                prods[i] = gated(*units[i], i < V_TURNS)
            for step, t, engine in W3_PLAN:
                if step == i:
                    prepare_w3(t, engine)
            if i >= LAG:
                t, hf = units[i - LAG]
                finish_h(t, hf, prods[i - LAG])
                if hf == HALVES - 1:
                    pick(t)

        x1_bf = held([P, NP * PACK], BF16, "x1_bf", tag="last")
        x1_codes = held([P, NP], U32, "x1_codes")
        x1_scale = held([P, NP], U8, "x1_scale")
        tiles = NP // P
        for m in range(tiles):
            nc.scalar.copy(
                out=x1_bf[:, m * P * PACK : (m + 1) * P * PACK].rearrange("p (c i t) -> p c t i", i=4, t=PACK),
                in_=x1_rows[:, :, m * P : (m + 1) * P].rearrange("p t (c i) -> p c t i", i=4),
            )

        def quantize_x1(m0, m1):
            nc.vector.quantize_mx(
                out=x1_codes[:, m0 * P : m1 * P].bitcast(FP8X4),
                scales=x1_scale[:, m0 * P : m1 * P],
                in_=x1_bf[:, m0 * P * PACK : m1 * P * PACK],
            )

        quantize_x1(0, 1)
        nc.vector.quantize_mx(out=x2_codes[:].bitcast(FP8X4), scales=x2_scale[:], in_=x2_bf[:])
        quantize_x1(1, 2)
        quantize_x1(2, tiles)
        for m in range(tiles):
            e_ps = psum.tile([P, BANK], F32, name="acc_w1", tag="acc_w1", bufs=BUF_A)
            nc.tensor.matmul_mx(
                out=e_ps[:],
                lhsT=x1_codes[:, m * P : (m + 1) * P].bitcast(FP8X4),
                lhsT_scale=x1_scale[:, m * P : (m + 1) * P],
                rhs=x2_codes[:].bitcast(FP8X4),
                rhs_scale=x2_scale[:],
                start=True,
                stop=True,
            )
            shifted = ring.tile([P, NP], F32, name="shifted", bufs=4)
            score = ring.tile([P, NP], F32, name="score", bufs=4)
            width = NP if m < tiles - 1 else NP // 2
            for c0 in range(0, NP, width):
                cols = slice(c0, c0 + width)
                nc.vector.tensor_tensor(out=shifted[:, cols], in0=e_ps[:, cols], in1=board_sb[:, cols], op=ALU.add)
                nc.scalar.activation(out=score[:, cols], in_=shifted[:, cols], func=ACT.Tanh)
                nc.sync.dma_start(out=out[m * P : (m + 1) * P, cols], in_=score[:, cols])
